import numpy as np
CORES = [34,162,290,418,42,426]
N = 6
R, T, B = 4096, 2048, 128
def entries(a): return a.T.reshape(-1)
def pack(v, P): return np.ascontiguousarray(np.asarray(v, np.int32).reshape(-1, P).T)
def lists(rng, how):
    I = rng.integers(0, N * R, (N, T)); E = np.sort(rng.integers(0, T + 1, (N, B)), axis=1)
    if how == "void":
        E = np.zeros((N, B), np.int64)
        for r in range(N): k = np.sort(1 + rng.permutation(B - 2)[:6]); c = np.sort(1 + rng.permutation(T)[:6]); E[r] = np.concatenate([[0], c])[np.searchsorted(k, np.arange(B), side="right")]
        E[rng.integers(N)] = 0
    if how == "one":
        p = rng.permutation(N); z = rng.integers(0, B, N); z[p[0]] = 0; z[p[1]] = B - 1; E = np.where(np.arange(B)[None, :] < z[:, None], 0, T)
        I[p[::2]] = R * p[1] + I[p[::2]] % R
    if how == "single": E = np.broadcast_to(1 + np.arange(B), (N, B)).copy()
    if how == "hotrank": I = R * int(rng.integers(N)) + rng.integers(0, R, (N, T))
    if how == "edge":
        for r in range(N): I[r, rng.permutation(T)[:8 * N]] = np.tile(np.concatenate([R * np.arange(N), R * np.arange(N) + R - 1]), 4)
        E[:, -1] = T
    return {"idx": np.stack([pack(i, 16) for i in I]), "end": np.stack([pack(v, 16) for v in E])}
def setup_inputs(rng):
    return dict({"tab": rng.standard_normal((N, 128, R), dtype=np.float32)}, **lists(rng, "uniform"))
def setup_inputs_edge(rng):
    d = setup_inputs(rng); d.update(lists(rng, "edge"))
    for k in ("tab",): d[k] = (d[k].astype(np.float32) * 1024.0).astype(d[k].dtype)
    return d
def setup_inputs_hotrank(rng):
    d = setup_inputs(rng); d.update(lists(rng, "hotrank"))
    for k in ("tab",): d[k] = (d[k].astype(np.float32) * (1 / 1024.0)).astype(d[k].dtype)
    return d
def setup_inputs_one(rng):
    d = setup_inputs(rng); d.update(lists(rng, "one"))
    return d
def setup_inputs_single(rng):
    d = setup_inputs(rng); d.update(lists(rng, "single"))
    return d
def setup_inputs_void(rng):
    d = setup_inputs(rng); d.update(lists(rng, "void"))
    return d
def check_inputs(x):
    bad = []
    if x["idx"].min() < 0 or x["idx"].max() >= N * R: bad.append("idx out of range")
    if x["end"].min() < 0 or x["end"].max() >= T + 1: bad.append("end out of range")
    if any((np.diff(entries(a)) < 0).any() for a in x["end"]): bad.append("end falls")
    return bad
def reference(tab, idx, end):
    A = np.concatenate(list(tab), axis=1).astype(np.float64)
    y = np.zeros((N, 128, B), np.float64)
    for r in range(N):
        G = A[:, entries(idx[r])]; c = np.concatenate([[0], entries(end[r])])
        for b in range(B):
            if c[b + 1] > c[b]: y[r][:, b] = G[:, c[b]:c[b + 1]].sum(axis=1)
    return {"y": y.astype(np.float32)}

@@ -1,0 +1,181 @@
+from concourse.bass import DstId, RemoteDMATransfer
+from concourse.mybir import dt, AluOpType, ActivationFunctionType
+
+N, R, NT, NB = 6, 4096, 2048, 128
+LW = 144
+PAD = 4
+SPLIT = 104
+GZ, S0 = 0, NT + 1
+WW = NT + 1 + NT // 2 + 1
+
+SCRATCH = {
+    "win": ("sbuf", [128, R + 2 * PAD], "float32"),
+    "idxi": ("sbuf", [128, 128], "int32"),
+    "endi": ("sbuf", [128, 8], "int32"),
+    "odd": ("sbuf", [128, 8], "int32"),
+    "pk": ("sbuf", [128, 16], "int32"),
+    "ones": ("sbuf", [128, 128], "float32"),
+    "ident": ("sbuf", [128, 128], "float32"),
+    "dsum": ("sbuf", [128, NB + 1], "float32"),
+    "yt": ("sbuf", [128, NB], "float32"),
+    "acc": ("psum", [128, NB], "float32"),
+}
+SEMAPHORES = ["lde", "ldi", "tab0", "tab1", "go", "z", "zo", "idn", "pa", "pm", "mine", "ls", "acs", "fin", "yr", "ys"]
+for _q in range(N):
+    SCRATCH["L%d" % _q] = ("sbuf", [128, LW], "uint16")
+    SCRATCH["off%d" % _q] = ("sbuf", [128, 128], "uint16")
+    SCRATCH["W%d" % _q] = ("sbuf", [128, WW], "float32")
+    SCRATCH["e%d" % _q] = ("sbuf", [128, NB], "float32")
+    SCRATCH["D%d" % _q] = ("sbuf", [128, NB], "float32")
+    SCRATCH["par%d" % _q] = ("sbuf", [128, NB], "float32")
+    SCRATCH["br%d" % _q] = ("sbuf", [128, NB], "float32")
+    SEMAPHORES += ["%s%d" % (s, _q) for s in ("L", "cv", "sg", "vg", "sc", "eo", "d", "par", "br")]
+
+
+def rank_program(g, core, T, topo):
+    me = T.rank_of(core)
+    if me is None:
+        return
+    cores, sem, A = T.cores, T.sem, AluOpType
+
+    def rackof(c):
+        return topo.rack(topo.host(c))
+
+    def partner_of(q):
+        c = cores[q]
+        return [k for k, d in enumerate(cores)
+                if rackof(d) != rackof(c) and topo.chip(d) == topo.chip(c) and topo.may_write(c, d)][0]
+
+    rack = [k for k, d in enumerate(cores) if rackof(d) == rackof(core)]
+    at = rack.index(me)
+    a, b = rack[(at + 1) % 3], rack[(at + 2) % 3]
+    p, fa, fb = partner_of(me), partner_of(a), partner_of(b)
+    order = [a, fa, fb, p, b, me]
+
+    def did(q):
+        rid, pid = topo.addr(cores[q], core)
+        return DstId(rid=rid, pnc=pid)
+
+    def send(qs, srcs, dst, rsem):
+        m = topo.mask(core, cores[qs[0]])
+        for q in qs:
+            m &= topo.mask(core, cores[q])
+        g.remote_dma_fused([RemoteDMATransfer(dst_ids=[did(q) for q in qs], dma_engine_mask=m, remote_sem=rsem,
+                                              srcs=srcs, dsts=[dst] * len(qs), alu_op=1 if len(srcs) > 1 else 0)],
+                           local_sem=sem.ls)
+        return bin(m).count("1")
+
+    def eng(q):
+        return bin(topo.mask(cores[q], core)).count("1")
+
+    v, s, sy = g.vector, g.scalar, g.sync
+    mine = T["L%d" % me]
+
+    for k in range(8):
+        (sy if k % 2 == 0 else s).dma_start(T.endi[16 * k:16 * k + 16, :], T.end[:, :]).then_inc(sem.lde, 16)
+    for k in range(8):
+        (sy if k % 2 == 0 else s).dma_start(T.idxi[16 * k:16 * k + 16, :], T.idx[:, :]).then_inc(sem.ldi, 16)
+    H = R // 2
+    sy.dma_start(T.win[:, PAD:PAD + H], T.tab[:, 0:H]).then_inc(sem.tab0, 16)
+    sy.wait_ge(sem.go, 1)
+    sy.dma_start(T.win[:, PAD + H:PAD + R], T.tab[:, H:R]).then_inc(sem.tab1, 16)
+
+    v.memset(T.ones[:], 1.0).then_inc(sem.zo, 1)
+    nz = 0
+    zs = [T.win[:, 0:PAD], T.win[:, PAD + R:], T.dsum[:, 0:1]]
+    for q in range(N):
+        zs += [T["W%d" % q][:, GZ:GZ + 1], T["W%d" % q][:, S0:S0 + 1]]
+    for z in zs:
+        v.memset(z, 0.0).then_inc(sem.z, 1)
+        nz += 1
+    g.wait_ge(sem.zo, 1)
+    g.affine_select(T.ident[:], T.ones[:], [[-1, 128]], A.is_equal, 0.0, 0, 1).then_inc(sem.idn, 1)
+
+    v.wait_ge(sem.lde, 128)
+    v.tensor_scalar(T.odd[:], T.endi[:], 1, None, A.bitwise_and).then_inc(sem.pa, 1)
+    v.tensor_scalar(T.pk[:, 0:8], T.endi[:], 1, None, A.arith_shift_right).then_inc(sem.pm, 1)
+    v.wait_ge(sem.pa, 1)
+    v.tensor_tensor(T.pk[:, 8:16], T.endi[:], T.odd[:], A.mult).then_inc(sem.pm, 1)
+    v.wait_ge(sem.ldi, 128)
+    v.tensor_copy(mine[:, 0:128], T.idxi[:]).then_inc(sem.mine, 1)
+    v.wait_ge(sem.pm, 2)
+    v.tensor_copy(mine[:, 128:144], T.pk[:]).then_inc(sem.mine, 1)
+
+    nl = 0
+    g.wait_ge(sem.mine, 2)
+    nl += send([a, b, p], [mine[:]], mine[:], sem["L%d" % me])
+    g.sem_inc(sem.go, 1)
+    LP = T["L%d" % p]
+    g.wait_ge(sem["L%d" % p], eng(p))
+    nl += send([a, b], [LP[:]], LP[:], sem["L%d" % p])
+
+    winw = T.win[:, PAD - 1:PAD + R + 1]
+    v.wait_ge(sem.z, nz)
+    v.wait_ge(sem.mine, 2)
+
+    def conv(q):
+        if q != me:
+            v.wait_ge(sem["L%d" % q], eng(q if q in rack or q == p else partner_of(q)))
+        v.tensor_scalar(T["off%d" % q][:], T["L%d" % q][:, 0:128], float(1 - R * me), float(R + 1),
+                        A.add, A.min).then_inc(sem["cv%d" % q], 1)
+
+    def dma_of_table(queue):
+        queue.wait_ge(sem.tab0, 16)
+        queue.wait_ge(sem.tab1, 16)
+
+    s.wait_ge(sem.z, nz)
+    for i, q in enumerate(order):
+        off, W = T["off%d" % q], T["W%d" % q]
+        s.wait_ge(sem["cv%d" % q], 1)
+        if i == 0:
+            dma_of_table(s)
+        s.activation(W[:, 1:1 + 16 * SPLIT], winw.indirect(off[:, 0:SPLIT]),
+                     ActivationFunctionType.Copy).then_inc(sem["sg%d" % q], 1)
+
+    conv(me)
+    conv(a)
+    for i, q in enumerate(order):
+        L, off, W = T["L%d" % q], T["off%d" % q], T["W%d" % q]
+        E, D = T["e%d" % q], T["D%d" % q]
+        v.wait_ge(sem["cv%d" % q], 1)
+        if i == 0:
+            dma_of_table(v)
+        v.tensor_copy(W[:, 1 + 16 * SPLIT:1 + NT], winw.indirect(off[:, SPLIT:128])).then_inc(sem["vg%d" % q], 1)
+        if i + 1 < len(order) and order[i + 1] != me:
+            conv(order[i + 1])
+        v.wait_ge(sem["vg%d" % q], 1)
+        v.wait_ge(sem["sg%d" % q], 1)
+        v.tensor_tensor_scan(W[:, S0 + 1:S0 + 1 + NT // 2], W[:, 1:1 + NT:2], W[:, 2:2 + NT - 1:2], 0.0,
+                             A.add, A.add).then_inc(sem["sc%d" % q], 1)
+        v.tensor_copy(E[:], W[:, GZ:GZ + NT + 1].indirect(L[:, 136:144])).then_inc(sem["eo%d" % q], 1)
+        v.wait_ge(sem["sc%d" % q], 1)
+        v.wait_ge(sem["eo%d" % q], 1)
+        v.tensor_tensor(D[:], W[:, S0:S0 + NT // 2 + 1].indirect(L[:, 128:136]), E[:], A.add).then_inc(sem["d%d" % q], 1)
+
+    for q in order[:-1]:
+        D = T["D%d" % q]
+        g.wait_ge(sem["d%d" % q], 1)
+        if q in rack:
+            nl += send([q], [D[:]], T["par%d" % me][:], sem["par%d" % me])
+        elif q == p:
+            for k in (a, b):
+                g.wait_ge(sem["br%d" % k], eng(k))
+            nl += send([p], [D[:], T["br%d" % a][:], T["br%d" % b][:]], T["par%d" % me][:], sem["par%d" % me])
+        else:
+            nl += send([partner_of(q)], [D[:]], T["br%d" % me][:], sem["br%d" % me])
+
+    srcs = [b, p, a]
+    g.tensor.wait_ge(sem.idn, 1)
+    for i, q in enumerate(srcs):
+        g.tensor.wait_ge(sem["par%d" % q], eng(q))
+        g.tensor.matmul(T.acc[:], T.ident[:], T["par%d" % q][:], i == 0, i == 2).then_inc(sem.acs, 1)
+
+    v.wait_ge(sem["d%d" % me], 1)
+    v.wait_ge(sem.acs, 3)
+    v.tensor_tensor(T.dsum[:, 1:1 + NB], T["D%d" % me][:], T.acc[:], A.add).then_inc(sem.fin, 1)
+    v.wait_ge(sem.fin, 1)
+    v.tensor_tensor(T.yt[:], T.dsum[:, 1:1 + NB], T.dsum[:, 0:NB], A.subtract).then_inc(sem.yr, 1)
+    sy.wait_ge(sem.yr, 1)
+    sy.dma_start(T.y[:, :], T.yt[:]).then_inc(sem.ys, 16)
+    sy.wait_ge(sem.ys, 16)
+    g.wait_ge(sem.ls, nl)

@@ -4,9 +4,15 @@ from concourse.mybir import dt, AluOpType, ActivationFunctionType
 N, R, NT, NB = 6, 4096, 2048, 128
 LW = 144
 PAD = 4
-SPLIT = 104
 GZ, S0 = 0, NT + 1
 WW = NT + 1 + NT // 2 + 1
+LOADS = [2304, 1792]
+PIECES = [1024, 1024, 1024, 1024]
+ORDER = ["fa", "fb", "p", "me"]
+GATE = ["b", "a"]
+FILL = (24, 40)
+SPLIT = [80, 92, 116, 100]
+SPLIT_G = [72, 92]
 
 SCRATCH = {
     "win": ("sbuf", [128, R + 2 * PAD], "float32"),
@@ -16,11 +22,13 @@ SCRATCH = {
     "pk": ("sbuf", [128, 16], "int32"),
     "ones": ("sbuf", [128, 128], "float32"),
     "ident": ("sbuf", [128, 128], "float32"),
+    "part": ("sbuf", [128, NB], "float32"),
     "dsum": ("sbuf", [128, NB + 1], "float32"),
     "yt": ("sbuf", [128, NB], "float32"),
     "acc": ("psum", [128, NB], "float32"),
 }
-SEMAPHORES = ["lde", "ldi", "tab0", "tab1", "go", "z", "zo", "idn", "pa", "pm", "mine", "ls", "acs", "fin", "yr", "ys"]
+SEMAPHORES = ["lde", "ldi", "go", "z", "zo", "idn", "pa", "pm", "mine", "ls", "acs", "prt", "fin", "yr", "ys"]
+SEMAPHORES += ["tab%d" % k for k in range(len(LOADS))] + ["pc%d" % k for k in range(len(PIECES))]
 for _q in range(N):
     SCRATCH["L%d" % _q] = ("sbuf", [128, LW], "uint16")
     SCRATCH["off%d" % _q] = ("sbuf", [128, 128], "uint16")
@@ -33,10 +41,12 @@ for _q in range(N):
 
 
 def rank_program(g, core, T, topo):
-    me = T.rank_of(core)
-    if me is None:
-        return
     cores, sem, A = T.cores, T.sem, AluOpType
+    homes = [k for k, c in enumerate(cores)
+             if topo.host(c) == topo.host(core) and topo.chip(c) == topo.chip(core) and topo.die(c) == topo.die(core)]
+    if not homes:
+        return
+    me = homes[0]
 
     def rackof(c):
         return topo.rack(topo.host(c))
@@ -46,105 +56,174 @@ def rank_program(g, core, T, topo):
         return [k for k, d in enumerate(cores)
                 if rackof(d) != rackof(c) and topo.chip(d) == topo.chip(c) and topo.may_write(c, d)][0]
 
-    rack = [k for k, d in enumerate(cores) if rackof(d) == rackof(core)]
-    at = rack.index(me)
-    a, b = rack[(at + 1) % 3], rack[(at + 2) % 3]
-    p, fa, fb = partner_of(me), partner_of(a), partner_of(b)
-    order = [a, fa, fb, p, b, me]
+    def near(k):
+        r = [j for j, d in enumerate(cores) if rackof(d) == rackof(cores[k])]
+        i = r.index(k)
+        return r[(i + 1) % 3], r[(i + 2) % 3]
 
-    def did(q):
-        rid, pid = topo.addr(cores[q], core)
+    def gate_of(k):
+        c, want = cores[k], near(k) + (partner_of(k),)
+        return [d for d in range(512) if d != c and topo.host(d) == topo.host(c) and topo.chip(d) == topo.chip(c)
+                and topo.die(d) == topo.die(c) and all(topo.may_write(d, cores[j]) for j in want)][0]
+
+    def named(k):
+        x, y = near(k)
+        return {"a": x, "b": y, "fa": partner_of(x), "fb": partner_of(y), "p": partner_of(k), "me": k}
+
+    def where(q, k):
+        return gate_of(k) if q in [named(k)[n] for n in GATE] else cores[k]
+
+    hub, gate = cores[me], gate_of(me)
+    if core not in (hub, gate):
+        return
+    a, b = near(me)
+    p = partner_of(me)
+    v, s, sy = g.vector, g.scalar, g.sync
+    nl = [0]
+
+    def did(c):
+        rid, pid = topo.addr(c, core)
         return DstId(rid=rid, pnc=pid)
 
-    def send(qs, srcs, dst, rsem):
-        m = topo.mask(core, cores[qs[0]])
-        for q in qs:
-            m &= topo.mask(core, cores[q])
-        g.remote_dma_fused([RemoteDMATransfer(dst_ids=[did(q) for q in qs], dma_engine_mask=m, remote_sem=rsem,
-                                              srcs=srcs, dsts=[dst] * len(qs), alu_op=1 if len(srcs) > 1 else 0)],
+    def send(cs, srcs, dst, rsem, m=None):
+        if m is None:
+            m = topo.mask(core, cs[0])
+            for c in cs:
+                m &= topo.mask(core, c)
+        g.remote_dma_fused([RemoteDMATransfer(dst_ids=[did(c) for c in cs], dma_engine_mask=m, remote_sem=rsem,
+                                              srcs=srcs, dsts=[dst] * len(cs), alu_op=1 if len(srcs) > 1 else 0)],
                            local_sem=sem.ls)
-        return bin(m).count("1")
+        nl[0] += bin(m).count("1")
 
-    def eng(q):
-        return bin(topo.mask(cores[q], core)).count("1")
+    def eng(c):
+        return bin(topo.mask(c, core)).count("1")
 
-    v, s, sy = g.vector, g.scalar, g.sync
-    mine = T["L%d" % me]
+    few = topo.mask(hub, gate_of(p)) & topo.mask(hub, gate)
+    pieces, col = [], PAD
+    for n in PIECES:
+        pieces.append((col + n, T.win[:, col:col + n]))
+        col += n
 
-    for k in range(8):
-        (sy if k % 2 == 0 else s).dma_start(T.endi[16 * k:16 * k + 16, :], T.end[:, :]).then_inc(sem.lde, 16)
-    for k in range(8):
-        (sy if k % 2 == 0 else s).dma_start(T.idxi[16 * k:16 * k + 16, :], T.idx[:, :]).then_inc(sem.ldi, 16)
-    H = R // 2
-    sy.dma_start(T.win[:, PAD:PAD + H], T.tab[:, 0:H]).then_inc(sem.tab0, 16)
-    sy.wait_ge(sem.go, 1)
-    sy.dma_start(T.win[:, PAD + H:PAD + R], T.tab[:, H:R]).then_inc(sem.tab1, 16)
+    mine, pm, lm = T["L%d" % me], T["par%d" % me], sem["L%d" % me]
+    if core == hub:
+        lists = [named(me)[n] for n in ORDER]
+        split = dict(zip(lists, SPLIT))
+        for k in range(8):
+            (sy if k % 2 == 0 else s).dma_start(T.endi[16 * k:16 * k + 16, :], T.end[:, :]).then_inc(sem.lde, 16)
+        for k in range(8):
+            (sy if k % 2 == 0 else s).dma_start(T.idxi[16 * k:16 * k + 16, :], T.idx[:, :]).then_inc(sem.ldi, 16)
+        c0 = 0
+        for k, n in enumerate(LOADS):
+            if k == 1:
+                sy.wait_ge(sem.go, 1)
+            sy.dma_start(T.win[:, PAD + c0:PAD + c0 + n], T.tab[:, c0:c0 + n]).then_inc(sem["tab%d" % k], 16)
+            c0 += n
+        v.memset(T.ones[:], 1.0).then_inc(sem.zo, 1)
+        g.wait_ge(sem.zo, 1)
+        g.affine_select(T.ident[:], T.ones[:], [[-1, 128]], A.is_equal, 0.0, 0, 1).then_inc(sem.idn, 1)
 
-    v.memset(T.ones[:], 1.0).then_inc(sem.zo, 1)
-    nz = 0
-    zs = [T.win[:, 0:PAD], T.win[:, PAD + R:], T.dsum[:, 0:1]]
-    for q in range(N):
+        v.wait_ge(sem.lde, 128)
+        v.tensor_scalar(T.odd[:], T.endi[:], 1, None, A.bitwise_and).then_inc(sem.pa, 1)
+        v.tensor_scalar(T.pk[:, 0:8], T.endi[:], 1, None, A.arith_shift_right).then_inc(sem.pm, 1)
+        v.wait_ge(sem.pa, 1)
+        v.tensor_tensor(T.pk[:, 8:16], T.endi[:], T.odd[:], A.mult).then_inc(sem.pm, 1)
+        v.wait_ge(sem.ldi, 128)
+        v.tensor_copy(mine[:, 0:128], T.idxi[:]).then_inc(sem.mine, 1)
+        v.wait_ge(sem.pm, 2)
+        v.tensor_copy(mine[:, 128:144], T.pk[:]).then_inc(sem.mine, 1)
+
+        g.wait_ge(sem.mine, 2)
+        send([gate], [mine[:]], mine[:], lm, few)
+        send([gate_of(p)], [mine[:]], mine[:], lm)
+        g.sem_inc(sem.go, 1)
+        got = 0
+        for i, (c, w) in enumerate(pieces):
+            while PAD + sum(LOADS[:got]) < c:
+                g.wait_ge(sem["tab%d" % got], 16)
+                got += 1
+            send([gate], [w], w, sem["pc%d" % i])
+    else:
+        lists = [named(me)[n] for n in GATE]
+        split = dict(zip(lists, SPLIT_G))
+        g.wait_ge(lm, bin(few).count("1"))
+        send([where(me, a), where(me, b)], [mine[:]], mine[:], lm)
+        LP = T["L%d" % p]
+        g.wait_ge(sem["L%d" % p], eng(cores[p]))
+        send([cores[b], cores[a]], [LP[:]], LP[:], sem["L%d" % p])
+        send([hub], [LP[:]], LP[:], sem["L%d" % p])
+
+    zs = [T.win[:, 0:PAD], T.win[:, PAD + R:]]
+    if core == hub:
+        zs.append(T.dsum[:, 0:1])
+    for q in lists:
         zs += [T["W%d" % q][:, GZ:GZ + 1], T["W%d" % q][:, S0:S0 + 1]]
     for z in zs:
         v.memset(z, 0.0).then_inc(sem.z, 1)
-        nz += 1
-    g.wait_ge(sem.zo, 1)
-    g.affine_select(T.ident[:], T.ones[:], [[-1, 128]], A.is_equal, 0.0, 0, 1).then_inc(sem.idn, 1)
-
-    v.wait_ge(sem.lde, 128)
-    v.tensor_scalar(T.odd[:], T.endi[:], 1, None, A.bitwise_and).then_inc(sem.pa, 1)
-    v.tensor_scalar(T.pk[:, 0:8], T.endi[:], 1, None, A.arith_shift_right).then_inc(sem.pm, 1)
-    v.wait_ge(sem.pa, 1)
-    v.tensor_tensor(T.pk[:, 8:16], T.endi[:], T.odd[:], A.mult).then_inc(sem.pm, 1)
-    v.wait_ge(sem.ldi, 128)
-    v.tensor_copy(mine[:, 0:128], T.idxi[:]).then_inc(sem.mine, 1)
-    v.wait_ge(sem.pm, 2)
-    v.tensor_copy(mine[:, 128:144], T.pk[:]).then_inc(sem.mine, 1)
-
-    nl = 0
-    g.wait_ge(sem.mine, 2)
-    nl += send([a, b, p], [mine[:]], mine[:], sem["L%d" % me])
-    g.sem_inc(sem.go, 1)
-    LP = T["L%d" % p]
-    g.wait_ge(sem["L%d" % p], eng(p))
-    nl += send([a, b], [LP[:]], LP[:], sem["L%d" % p])
 
     winw = T.win[:, PAD - 1:PAD + R + 1]
-    v.wait_ge(sem.z, nz)
-    v.wait_ge(sem.mine, 2)
+    v.wait_ge(sem.z, len(zs))
+    s.wait_ge(sem.z, len(zs))
+    f1, f2 = FILL if core == hub else (0, 0)
 
     def conv(q):
-        if q != me:
-            v.wait_ge(sem["L%d" % q], eng(q if q in rack or q == p else partner_of(q)))
+        if q == me:
+            v.wait_ge(sem.mine, 2)
+        elif q in (a, b):
+            v.wait_ge(sem["L%d" % q], eng(gate_of(q)))
+        else:
+            v.wait_ge(sem["L%d" % q], eng(gate if q == p else gate_of(partner_of(q))))
         v.tensor_scalar(T["off%d" % q][:], T["L%d" % q][:, 0:128], float(1 - R * me), float(R + 1),
                         A.add, A.min).then_inc(sem["cv%d" % q], 1)
 
-    def dma_of_table(queue):
-        queue.wait_ge(sem.tab0, 16)
-        queue.wait_ge(sem.tab1, 16)
+    def table(queue):
+        if core == hub:
+            for k in range(len(LOADS)):
+                queue.wait_ge(sem["tab%d" % k], 16)
+        else:
+            for i in range(len(pieces)):
+                queue.wait_ge(sem["pc%d" % i], eng(hub))
 
-    s.wait_ge(sem.z, nz)
-    for i, q in enumerate(order):
-        off, W = T["off%d" % q], T["W%d" % q]
-        s.wait_ge(sem["cv%d" % q], 1)
-        if i == 0:
-            dma_of_table(s)
-        s.activation(W[:, 1:1 + 16 * SPLIT], winw.indirect(off[:, 0:SPLIT]),
+    def sgather(q, c0, c1):
+        s.activation(T["W%d" % q][:, 1 + 16 * c0:1 + 16 * c1], winw.indirect(T["off%d" % q][:, c0:c1]),
                      ActivationFunctionType.Copy).then_inc(sem["sg%d" % q], 1)
 
-    conv(me)
-    conv(a)
-    for i, q in enumerate(order):
-        L, off, W = T["L%d" % q], T["off%d" % q], T["W%d" % q]
-        E, D = T["e%d" % q], T["D%d" % q]
-        v.wait_ge(sem["cv%d" % q], 1)
-        if i == 0:
-            dma_of_table(v)
-        v.tensor_copy(W[:, 1 + 16 * SPLIT:1 + NT], winw.indirect(off[:, SPLIT:128])).then_inc(sem["vg%d" % q], 1)
-        if i + 1 < len(order) and order[i + 1] != me:
-            conv(order[i + 1])
-        v.wait_ge(sem["vg%d" % q], 1)
-        v.wait_ge(sem["sg%d" % q], 1)
+    def vgather(q, c0, c1):
+        v.tensor_copy(T["W%d" % q][:, 1 + 16 * c0:1 + 16 * c1],
+                      winw.indirect(T["off%d" % q][:, c0:c1])).then_inc(sem["vg%d" % q], 1)
+
+    if f1:
+        s.wait_ge(sem["cv%d" % me], 1)
+        table(s)
+        sgather(me, 0, f1)
+    for i, q in enumerate(lists):
+        s.wait_ge(sem["cv%d" % q], 1)
+        if i == 0 and not f1:
+            table(s)
+        sgather(q, f2 if q == me else 0, split[q])
+
+    if f1:
+        conv(me)
+        v.wait_ge(sem["cv%d" % me], 1)
+        table(v)
+        vgather(me, f1, f2)
+        conv(lists[0])
+    else:
+        conv(lists[0])
+        table(v)
+    v.wait_ge(sem["cv%d" % lists[0]], 1)
+    vgather(lists[0], split[lists[0]], 128)
+    conv(lists[1])
+    for i, q in enumerate(lists):
+        L, W, E, D = T["L%d" % q], T["W%d" % q], T["e%d" % q], T["D%d" % q]
+        if i + 1 < len(lists):
+            n = lists[i + 1]
+            v.wait_ge(sem["cv%d" % n], 1)
+            vgather(n, split[n], 128)
+            if i + 2 < len(lists) and not (f1 and lists[i + 2] == me):
+                conv(lists[i + 2])
+        parts = 2 if f1 and q == me else 1
+        v.wait_ge(sem["vg%d" % q], parts)
+        v.wait_ge(sem["sg%d" % q], parts)
         v.tensor_tensor_scan(W[:, S0 + 1:S0 + 1 + NT // 2], W[:, 1:1 + NT:2], W[:, 2:2 + NT - 1:2], 0.0,
                              A.add, A.add).then_inc(sem["sc%d" % q], 1)
         v.tensor_copy(E[:], W[:, GZ:GZ + NT + 1].indirect(L[:, 136:144])).then_inc(sem["eo%d" % q], 1)
@@ -152,30 +231,38 @@ def rank_program(g, core, T, topo):
         v.wait_ge(sem["eo%d" % q], 1)
         v.tensor_tensor(D[:], W[:, S0:S0 + NT // 2 + 1].indirect(L[:, 128:136]), E[:], A.add).then_inc(sem["d%d" % q], 1)
 
-    for q in order[:-1]:
+    for q in lists:
+        if q == me:
+            continue
         D = T["D%d" % q]
         g.wait_ge(sem["d%d" % q], 1)
-        if q in rack:
-            nl += send([q], [D[:]], T["par%d" % me][:], sem["par%d" % me])
+        if q in (a, b):
+            send([cores[q]], [D[:]], pm[:], sem["par%d" % me])
         elif q == p:
             for k in (a, b):
-                g.wait_ge(sem["br%d" % k], eng(k))
-            nl += send([p], [D[:], T["br%d" % a][:], T["br%d" % b][:]], T["par%d" % me][:], sem["par%d" % me])
+                g.wait_ge(sem["br%d" % k], eng(cores[k]))
+            send([cores[p]], [D[:], T["br%d" % a][:], T["br%d" % b][:]], pm[:], sem["par%d" % me])
         else:
-            nl += send([partner_of(q)], [D[:]], T["br%d" % me][:], sem["br%d" % me])
+            send([cores[partner_of(q)]], [D[:]], T["br%d" % me][:], sem["br%d" % me])
+    if core == gate:
+        g.wait_ge(sem.ls, nl[0])
+        return
 
-    srcs = [b, p, a]
+    ga, gb = where(me, a), where(me, b)
     g.tensor.wait_ge(sem.idn, 1)
-    for i, q in enumerate(srcs):
-        g.tensor.wait_ge(sem["par%d" % q], eng(q))
-        g.tensor.matmul(T.acc[:], T.ident[:], T["par%d" % q][:], i == 0, i == 2).then_inc(sem.acs, 1)
-
-    v.wait_ge(sem["d%d" % me], 1)
-    v.wait_ge(sem.acs, 3)
-    v.tensor_tensor(T.dsum[:, 1:1 + NB], T["D%d" % me][:], T.acc[:], A.add).then_inc(sem.fin, 1)
+    g.tensor.wait_ge(sem["par%d" % a], eng(ga))
+    g.tensor.matmul(T.acc[:], T.ident[:], T["par%d" % a][:], True, False).then_inc(sem.acs, 1)
+    g.tensor.wait_ge(sem["d%d" % me], 1)
+    g.tensor.matmul(T.acc[:], T.ident[:], T["D%d" % me][:], False, True).then_inc(sem.acs, 1)
+    v.wait_ge(sem.acs, 2)
+    v.wait_ge(sem["par%d" % b], eng(gb))
+    v.tensor_tensor(T.part[:], T["par%d" % b][:], T.acc[:], A.add).then_inc(sem.prt, 1)
+    v.wait_ge(sem.prt, 1)
+    v.wait_ge(sem["par%d" % p], eng(cores[p]))
+    v.tensor_tensor(T.dsum[:, 1:1 + NB], T.part[:], T["par%d" % p][:], A.add).then_inc(sem.fin, 1)
     v.wait_ge(sem.fin, 1)
     v.tensor_tensor(T.yt[:], T.dsum[:, 1:1 + NB], T.dsum[:, 0:NB], A.subtract).then_inc(sem.yr, 1)
     sy.wait_ge(sem.yr, 1)
     sy.dma_start(T.y[:, :], T.yt[:]).then_inc(sem.ys, 16)
     sy.wait_ge(sem.ys, 16)
-    g.wait_ge(sem.ls, nl)
+    g.wait_ge(sem.ls, nl[0])

from concourse.bass import DstId, RemoteDMATransfer
from concourse.mybir import dt, AluOpType, ActivationFunctionType

N, R, NT, NB = 6, 4096, 2048, 128
LW = 144
PAD = 4
GZ, S0 = 0, NT + 1
WW = NT + 1 + NT // 2 + 1
LOADS = [2304, 1792]
PIECES = [1024, 1024, 1024, 1024]
ORDER = ["fa", "fb", "p", "me"]
GATE = ["b", "a"]
FILL = (24, 40)
SPLIT = [80, 92, 116, 100]
SPLIT_G = [72, 92]

SCRATCH = {
    "win": ("sbuf", [128, R + 2 * PAD], "float32"),
    "idxi": ("sbuf", [128, 128], "int32"),
    "endi": ("sbuf", [128, 8], "int32"),
    "odd": ("sbuf", [128, 8], "int32"),
    "pk": ("sbuf", [128, 16], "int32"),
    "ones": ("sbuf", [128, 128], "float32"),
    "ident": ("sbuf", [128, 128], "float32"),
    "part": ("sbuf", [128, NB], "float32"),
    "dsum": ("sbuf", [128, NB + 1], "float32"),
    "yt": ("sbuf", [128, NB], "float32"),
    "acc": ("psum", [128, NB], "float32"),
}
SEMAPHORES = ["lde", "ldi", "go", "z", "zo", "idn", "pa", "pm", "mine", "ls", "acs", "prt", "fin", "yr", "ys"]
SEMAPHORES += ["tab%d" % k for k in range(len(LOADS))] + ["pc%d" % k for k in range(len(PIECES))]
for _q in range(N):
    SCRATCH["L%d" % _q] = ("sbuf", [128, LW], "uint16")
    SCRATCH["off%d" % _q] = ("sbuf", [128, 128], "uint16")
    SCRATCH["W%d" % _q] = ("sbuf", [128, WW], "float32")
    SCRATCH["e%d" % _q] = ("sbuf", [128, NB], "float32")
    SCRATCH["D%d" % _q] = ("sbuf", [128, NB], "float32")
    SCRATCH["par%d" % _q] = ("sbuf", [128, NB], "float32")
    SCRATCH["br%d" % _q] = ("sbuf", [128, NB], "float32")
    SEMAPHORES += ["%s%d" % (s, _q) for s in ("L", "cv", "sg", "vg", "sc", "eo", "d", "par", "br")]


def rank_program(g, core, T, topo):
    cores, sem, A = T.cores, T.sem, AluOpType
    homes = [k for k, c in enumerate(cores)
             if topo.host(c) == topo.host(core) and topo.chip(c) == topo.chip(core) and topo.die(c) == topo.die(core)]
    if not homes:
        return
    me = homes[0]

    def rackof(c):
        return topo.rack(topo.host(c))

    def partner_of(q):
        c = cores[q]
        return [k for k, d in enumerate(cores)
                if rackof(d) != rackof(c) and topo.chip(d) == topo.chip(c) and topo.may_write(c, d)][0]

    def near(k):
        r = [j for j, d in enumerate(cores) if rackof(d) == rackof(cores[k])]
        i = r.index(k)
        return r[(i + 1) % 3], r[(i + 2) % 3]

    def gate_of(k):
        c, want = cores[k], near(k) + (partner_of(k),)
        return [d for d in range(512) if d != c and topo.host(d) == topo.host(c) and topo.chip(d) == topo.chip(c)
                and topo.die(d) == topo.die(c) and all(topo.may_write(d, cores[j]) for j in want)][0]

    def named(k):
        x, y = near(k)
        return {"a": x, "b": y, "fa": partner_of(x), "fb": partner_of(y), "p": partner_of(k), "me": k}

    def where(q, k):
        return gate_of(k) if q in [named(k)[n] for n in GATE] else cores[k]

    hub, gate = cores[me], gate_of(me)
    if core not in (hub, gate):
        return
    a, b = near(me)
    p = partner_of(me)
    v, s, sy = g.vector, g.scalar, g.sync
    nl = [0]

    def did(c):
        rid, pid = topo.addr(c, core)
        return DstId(rid=rid, pnc=pid)

    def send(cs, srcs, dst, rsem, m=None):
        if m is None:
            m = topo.mask(core, cs[0])
            for c in cs:
                m &= topo.mask(core, c)
        g.remote_dma_fused([RemoteDMATransfer(dst_ids=[did(c) for c in cs], dma_engine_mask=m, remote_sem=rsem,
                                              srcs=srcs, dsts=[dst] * len(cs), alu_op=1 if len(srcs) > 1 else 0)],
                           local_sem=sem.ls)
        nl[0] += bin(m).count("1")

    def eng(c):
        return bin(topo.mask(c, core)).count("1")

    few = topo.mask(hub, gate_of(p)) & topo.mask(hub, gate)
    pieces, col = [], PAD
    for n in PIECES:
        pieces.append((col + n, T.win[:, col:col + n]))
        col += n

    mine, pm, lm = T["L%d" % me], T["par%d" % me], sem["L%d" % me]
    if core == hub:
        lists = [named(me)[n] for n in ORDER]
        split = dict(zip(lists, SPLIT))
        for k in range(8):
            (sy if k % 2 == 0 else s).dma_start(T.endi[16 * k:16 * k + 16, :], T.end[:, :]).then_inc(sem.lde, 16)
        for k in range(8):
            (sy if k % 2 == 0 else s).dma_start(T.idxi[16 * k:16 * k + 16, :], T.idx[:, :]).then_inc(sem.ldi, 16)
        c0 = 0
        for k, n in enumerate(LOADS):
            if k == 1:
                sy.wait_ge(sem.go, 1)
            sy.dma_start(T.win[:, PAD + c0:PAD + c0 + n], T.tab[:, c0:c0 + n]).then_inc(sem["tab%d" % k], 16)
            c0 += n
        v.memset(T.ones[:], 1.0).then_inc(sem.zo, 1)
        g.wait_ge(sem.zo, 1)
        g.affine_select(T.ident[:], T.ones[:], [[-1, 128]], A.is_equal, 0.0, 0, 1).then_inc(sem.idn, 1)

        v.wait_ge(sem.lde, 128)
        v.tensor_scalar(T.odd[:], T.endi[:], 1, None, A.bitwise_and).then_inc(sem.pa, 1)
        v.tensor_scalar(T.pk[:, 0:8], T.endi[:], 1, None, A.arith_shift_right).then_inc(sem.pm, 1)
        v.wait_ge(sem.pa, 1)
        v.tensor_tensor(T.pk[:, 8:16], T.endi[:], T.odd[:], A.mult).then_inc(sem.pm, 1)
        v.wait_ge(sem.ldi, 128)
        v.tensor_copy(mine[:, 0:128], T.idxi[:]).then_inc(sem.mine, 1)
        v.wait_ge(sem.pm, 2)
        v.tensor_copy(mine[:, 128:144], T.pk[:]).then_inc(sem.mine, 1)

        g.wait_ge(sem.mine, 2)
        send([gate], [mine[:]], mine[:], lm, few)
        send([gate_of(p)], [mine[:]], mine[:], lm)
        g.sem_inc(sem.go, 1)
        got = 0
        for i, (c, w) in enumerate(pieces):
            while PAD + sum(LOADS[:got]) < c:
                g.wait_ge(sem["tab%d" % got], 16)
                got += 1
            send([gate], [w], w, sem["pc%d" % i])
    else:
        lists = [named(me)[n] for n in GATE]
        split = dict(zip(lists, SPLIT_G))
        g.wait_ge(lm, bin(few).count("1"))
        send([where(me, a), where(me, b)], [mine[:]], mine[:], lm)
        LP = T["L%d" % p]
        g.wait_ge(sem["L%d" % p], eng(cores[p]))
        send([cores[b], cores[a]], [LP[:]], LP[:], sem["L%d" % p])
        send([hub], [LP[:]], LP[:], sem["L%d" % p])

    zs = [T.win[:, 0:PAD], T.win[:, PAD + R:]]
    if core == hub:
        zs.append(T.dsum[:, 0:1])
    for q in lists:
        zs += [T["W%d" % q][:, GZ:GZ + 1], T["W%d" % q][:, S0:S0 + 1]]
    for z in zs:
        v.memset(z, 0.0).then_inc(sem.z, 1)

    winw = T.win[:, PAD - 1:PAD + R + 1]
    v.wait_ge(sem.z, len(zs))
    s.wait_ge(sem.z, len(zs))
    f1, f2 = FILL if core == hub else (0, 0)

    def conv(q):
        if q == me:
            v.wait_ge(sem.mine, 2)
        elif q in (a, b):
            v.wait_ge(sem["L%d" % q], eng(gate_of(q)))
        else:
            v.wait_ge(sem["L%d" % q], eng(gate if q == p else gate_of(partner_of(q))))
        v.tensor_scalar(T["off%d" % q][:], T["L%d" % q][:, 0:128], float(1 - R * me), float(R + 1),
                        A.add, A.min).then_inc(sem["cv%d" % q], 1)

    def table(queue):
        if core == hub:
            for k in range(len(LOADS)):
                queue.wait_ge(sem["tab%d" % k], 16)
        else:
            for i in range(len(pieces)):
                queue.wait_ge(sem["pc%d" % i], eng(hub))

    def sgather(q, c0, c1):
        s.activation(T["W%d" % q][:, 1 + 16 * c0:1 + 16 * c1], winw.indirect(T["off%d" % q][:, c0:c1]),
                     ActivationFunctionType.Copy).then_inc(sem["sg%d" % q], 1)

    def vgather(q, c0, c1):
        v.tensor_copy(T["W%d" % q][:, 1 + 16 * c0:1 + 16 * c1],
                      winw.indirect(T["off%d" % q][:, c0:c1])).then_inc(sem["vg%d" % q], 1)

    if f1:
        s.wait_ge(sem["cv%d" % me], 1)
        table(s)
        sgather(me, 0, f1)
    for i, q in enumerate(lists):
        s.wait_ge(sem["cv%d" % q], 1)
        if i == 0 and not f1:
            table(s)
        sgather(q, f2 if q == me else 0, split[q])

    if f1:
        conv(me)
        v.wait_ge(sem["cv%d" % me], 1)
        table(v)
        vgather(me, f1, f2)
        conv(lists[0])
    else:
        conv(lists[0])
        table(v)
    v.wait_ge(sem["cv%d" % lists[0]], 1)
    vgather(lists[0], split[lists[0]], 128)
    conv(lists[1])
    for i, q in enumerate(lists):
        L, W, E, D = T["L%d" % q], T["W%d" % q], T["e%d" % q], T["D%d" % q]
        if i + 1 < len(lists):
            n = lists[i + 1]
            v.wait_ge(sem["cv%d" % n], 1)
            vgather(n, split[n], 128)
            if i + 2 < len(lists) and not (f1 and lists[i + 2] == me):
                conv(lists[i + 2])
        parts = 2 if f1 and q == me else 1
        v.wait_ge(sem["vg%d" % q], parts)
        v.wait_ge(sem["sg%d" % q], parts)
        v.tensor_tensor_scan(W[:, S0 + 1:S0 + 1 + NT // 2], W[:, 1:1 + NT:2], W[:, 2:2 + NT - 1:2], 0.0,
                             A.add, A.add).then_inc(sem["sc%d" % q], 1)
        v.tensor_copy(E[:], W[:, GZ:GZ + NT + 1].indirect(L[:, 136:144])).then_inc(sem["eo%d" % q], 1)
        v.wait_ge(sem["sc%d" % q], 1)
        v.wait_ge(sem["eo%d" % q], 1)
        v.tensor_tensor(D[:], W[:, S0:S0 + NT // 2 + 1].indirect(L[:, 128:136]), E[:], A.add).then_inc(sem["d%d" % q], 1)

    for q in lists:
        if q == me:
            continue
        D = T["D%d" % q]
        g.wait_ge(sem["d%d" % q], 1)
        if q in (a, b):
            send([cores[q]], [D[:]], pm[:], sem["par%d" % me])
        elif q == p:
            for k in (a, b):
                g.wait_ge(sem["br%d" % k], eng(cores[k]))
            send([cores[p]], [D[:], T["br%d" % a][:], T["br%d" % b][:]], pm[:], sem["par%d" % me])
        else:
            send([cores[partner_of(q)]], [D[:]], T["br%d" % me][:], sem["br%d" % me])
    if core == gate:
        g.wait_ge(sem.ls, nl[0])
        return

    ga, gb = where(me, a), where(me, b)
    g.tensor.wait_ge(sem.idn, 1)
    g.tensor.wait_ge(sem["par%d" % a], eng(ga))
    g.tensor.matmul(T.acc[:], T.ident[:], T["par%d" % a][:], True, False).then_inc(sem.acs, 1)
    g.tensor.wait_ge(sem["d%d" % me], 1)
    g.tensor.matmul(T.acc[:], T.ident[:], T["D%d" % me][:], False, True).then_inc(sem.acs, 1)
    v.wait_ge(sem.acs, 2)
    v.wait_ge(sem["par%d" % b], eng(gb))
    v.tensor_tensor(T.part[:], T["par%d" % b][:], T.acc[:], A.add).then_inc(sem.prt, 1)
    v.wait_ge(sem.prt, 1)
    v.wait_ge(sem["par%d" % p], eng(cores[p]))
    v.tensor_tensor(T.dsum[:, 1:1 + NB], T.part[:], T["par%d" % p][:], A.add).then_inc(sem.fin, 1)
    v.wait_ge(sem.fin, 1)
    v.tensor_tensor(T.yt[:], T.dsum[:, 1:1 + NB], T.dsum[:, 0:NB], A.subtract).then_inc(sem.yr, 1)
    sy.wait_ge(sem.yr, 1)
    sy.dma_start(T.y[:, :], T.yt[:]).then_inc(sem.ys, 16)
    sy.wait_ge(sem.ys, 16)
    g.wait_ge(sem.ls, nl[0])
